import numpy as np
import ml_dtypes


def mxq(x, axis, fmt="e4m3"):
    dtype, down = {"e4m3": (ml_dtypes.float8_e4m3fn, 7), "e5m2": (ml_dtypes.float8_e5m2, 14)}[fmt]
    v = np.moveaxis(np.asarray(x, np.float32).astype(ml_dtypes.bfloat16).astype(np.float64), axis, -1)
    blocks = v.reshape(v.shape[:-1] + (-1, 32))
    amax = np.abs(blocks).max(-1, keepdims=True)
    byte = np.maximum(np.where(amax > 0, np.frexp(amax)[1] - 1 + 127, 0) - down, 1)
    scale = np.exp2(byte - 127.0)
    codes = (blocks / scale).astype(np.float32).astype(dtype).astype(np.float64)
    return np.moveaxis((codes * scale).reshape(v.shape), -1, axis)


WIDE = False


def mx_kscale(k):
    if not WIDE:
        return np.ones(k)
    levels = np.array([30, -30])
    if k % 512:
        return np.exp2(np.random.permutation(np.resize(levels, k // 32))).repeat(32)
    a = np.empty((k // 512, 16))
    for p in range(k // 512):
        a[p, :8] = np.random.permutation(np.resize(levels, 8))
        for g in range(8):
            far = levels[np.abs(levels - a[p, g]) >= 10]
            a[p, g + 8] = far[np.random.randint(len(far))]
    return np.exp2(a.ravel()).repeat(32)


def f64(x):
    return np.asarray(x).astype(np.float64)


def striped(idx):
    return np.tile(np.asarray(idx).reshape(-1, 16).T, (8, 1)).astype(np.uint16)


def unstriped(offs):
    return offs[:16].T.reshape(-1).astype(np.int64)


E2M1 = np.array([0.0, 0.5, 1.0, 1.5, 2.0, 3.0, 4.0, 6.0, -0.0, -0.5, -1.0, -1.5, -2.0, -3.0, -4.0, -6.0])


def pack_weight(w, fmt):
    k, n = w.shape
    w = f64(np.asarray(w, np.float32).astype(ml_dtypes.bfloat16)).reshape(k // 32, 32, n)
    amax = np.abs(w).max(1)
    if fmt == "e4m3":
        byte = np.frexp(amax)[1] - 1 + 127 - 7
    else:
        mant, ex = np.frexp(amax / 6.0)
        byte = np.where(mant > 0.5, ex, ex - 1) + 127
    byte = np.clip(np.where(amax > 0, byte, 1), 1, 254)
    scaled = (w * np.exp2(127.0 - byte)[:, None, :]).reshape(k, n).astype(np.float32)
    by_word = np.ascontiguousarray(scaled.reshape(k // 512, 128, 4, n).transpose(0, 1, 3, 2))
    if fmt == "e4m3":
        words = by_word.astype(ml_dtypes.float8_e4m3fn).view(np.uint8)
    else:
        c = by_word.astype(ml_dtypes.float4_e2m1fn).view(np.uint8) & 0xF
        words = (c[..., 0::2] | (c[..., 1::2] << 4)).reshape(k // 512, 128, 2 * n)
    return np.ascontiguousarray(words), np.ascontiguousarray(byte.astype(np.uint8).reshape(k // 512, 16, n))


def unpack_weight(words, scales, fmt):
    g, _, n = scales.shape
    words = np.ascontiguousarray(words).reshape(g, 128, n, -1)
    if fmt == "e4m3":
        vals = words.view(ml_dtypes.float8_e4m3fn).astype(np.float64)
    else:
        nib = np.empty((g, 128, n, 4), np.uint8)
        nib[..., 0::2] = words & 0xF
        nib[..., 1::2] = words >> 4
        vals = E2M1[nib]
    vals = vals * np.repeat(np.exp2(scales.astype(np.float64) - 127.0), 8, axis=1)[..., None]
    return vals.transpose(0, 1, 3, 2).reshape(g * 512, n)


K, T, J, I, S, V = 1024, 1024, 256, 256, 512, 1024


def setup_inputs():
    n = np.random.standard_normal
    idx = np.random.permutation(T)[:J]
    idx2 = np.random.permutation(S)[:J]
    idx3 = np.random.permutation(V)[:I]
    fk = mx_kscale(K)
    kyp = pack_weight(n((K, V)) / fk[:, None], "e4m3")
    return {
        "xf": (n((K, T)) * 0.03).astype(np.float32),
        "xb": (n((K, S))).astype(np.float32),
        "fk": (np.random.uniform(0.5, 2.0, (K, 1)) * fk[:, None]).astype(np.float32),
        "ky_words": kyp[0],
        "ky_scales": kyp[1],
        "bi": (np.random.uniform(-0.7, 0.7, (1, I))).astype(np.float32),
        "offs": striped(idx),
        "offs2": striped(idx2),
        "offs3": striped(idx3),
    }


def reference(xf, xb, fk, ky_words, ky_scales, bi, offs, offs2, offs3):
    idx = unstriped(offs)
    idx2 = unstriped(offs2)
    idx3 = unstriped(offs3)
    kyu = unpack_weight(ky_words, ky_scales, "e4m3")
    u = f64(xf)[:, idx] * f64(xb)[:, idx2] * f64(fk)
    uq = mxq(u, 0, "e5m2")
    kyidx3g = kyu[:, idx3]
    a0 = uq.T @ kyidx3g
    a = a0 + f64(bi)
    mn = np.mean(a, axis=1, keepdims=True)
    y = np.maximum(a - mn, 0.0)
    return y

@@ -1,0 +1,143 @@
+from contextlib import ExitStack
+
+import concourse.mybir as mybir
+from concourse.masks import make_identity
+
+K, T, S, V, J, I = 1024, 1024, 512, 1024, 256, 256
+FLOPS = 2 * K * J * I
+
+F32 = mybir.dt.float32
+BF16 = mybir.dt.bfloat16
+I32 = mybir.dt.int32
+U32 = mybir.dt.uint32
+U16 = mybir.dt.uint16
+U8 = mybir.dt.uint8
+E4M3X4 = mybir.dt.float8_e4m3fn_x4
+E5M2X4 = mybir.dt.float8_e5m2_x4
+ALU = mybir.AluOpType
+ACT = mybir.ActivationFunctionType
+
+P = 128
+PACK = 4
+K_PASS = P * PACK
+PASSES = K // K_PASS
+HALVES = J // P
+QUADRANTS = 4
+SCALE_ROWS = 4
+
+
+def tile_list_scores_products_listed_abovemean_kernel(tc, xf, xb, fk, ky_words, ky_scales, bi, offs, offs2, offs3, out):
+    nc = tc.nc
+    with ExitStack() as ctx:
+        keep = ctx.enter_context(tc.tile_pool(name="keep", bufs=1))
+        psum = ctx.enter_context(tc.psum_pool(name="psum", bufs=1))
+
+        xf_list = keep.tile([P, J // 16], U16, name="xf_list")
+        xb_list = keep.tile([P, J // 16], U16, name="xb_list")
+        ky_list = keep.tile([P, I // 16], U16, name="ky_list")
+        factors = keep.tile([P, PASSES, 2 * PACK], F32, name="factors")
+        xb_rows = [keep.tile([P, PACK, S], F32, name="xb_rows%d" % z) for z in range(PASSES)]
+        xf_rows = [[keep.tile([P, T], F32, name="xf_rows%d_%d" % (z, r)) for r in range(PACK)] for z in range(PASSES)]
+        key_words = [keep.tile([P, V], I32, name="key_words%d" % z) for z in range(PASSES)]
+        key_scales = keep.tile([P, PASSES, V], U8, name="key_scales")
+        bias_pairs = keep.tile([P, 2], F32, name="bias_pairs")
+        identity = keep.tile([P, P], F32, name="identity")
+
+        xf_view = xf.rearrange("(z p r) t -> z r p t", z=PASSES, r=PACK)
+        xb_view = xb.rearrange("(z p r) s -> z p r s", z=PASSES, r=PACK)
+
+        nc.sync.dma_start(xb_rows[0][:], xb_view[0])
+        nc.sync.dma_start(xb_list[:], offs2)
+        nc.sync.dma_start(factors[:, :, 0:PACK], fk.rearrange("(z p r) o -> p z (r o)", z=PASSES, r=PACK))
+        nc.sync.dma_start(xf_rows[0][0][:], xf_view[0, 0])
+        nc.sync.dma_start(xf_list[:], offs)
+        for r in range(1, PACK):
+            nc.sync.dma_start(xf_rows[0][r][:], xf_view[0, r])
+        nc.sync.dma_start(xb_rows[1][:], xb_view[1])
+        nc.sync.dma_start(ky_list[:], offs3)
+        for r in range(PACK):
+            nc.sync.dma_start(xf_rows[1][r][:], xf_view[1, r])
+        for z in range(PASSES):
+            nc.sync.dma_start(key_words[z][:], ky_words[z].rearrange("p n r -> p (n r)").bitcast(I32))
+
+        nc.vector.memset(key_scales[:].rearrange("p z v -> p (z v)").bitcast(I32), 0)
+        for q in range(QUADRANTS):
+            nc.gpsimd.dma_start(
+                key_scales[32 * q : 32 * q + SCALE_ROWS].bitcast(I32),
+                ky_scales[:, SCALE_ROWS * q : SCALE_ROWS * (q + 1), :].rearrange("z r v -> r z v").bitcast(I32),
+            )
+        nc.gpsimd.dma_start(bias_pairs[:], bi.rearrange("o (p c) -> p (o c)", c=2))
+        make_identity(nc, identity[:])
+
+        bias_bank = psum.tile([P, 2, P], F32, name="bias_bank")
+        for c in range(2):
+            nc.tensor.transpose(bias_bank[:, c, :], bias_pairs[:, c : c + 1].to_broadcast([P, P]), identity[:])
+        bias_scaled = keep.tile([P, I], F32, name="bias_scaled")
+
+        acc = [psum.tile([P, I], F32, name="acc%d" % h) for h in range(HALVES)]
+        picked_scales = []
+        for z in range(PASSES):
+            product = keep.tile([P, PACK, J], F32, name="product%d" % z)
+            for r in range(PACK):
+                xb_picked = keep.tile([P, J], F32, name="xb_picked%d_%d" % (z, r))
+                nc.scalar.activation(xb_picked[:], xb_rows[z][:, r, :].indirect(xb_list[:]), ACT.Copy)
+                xb_scaled = keep.tile([P, J], F32, name="xb_scaled%d_%d" % (z, r))
+                nc.scalar.activation(xb_scaled[:], xb_picked[:], ACT.Copy, scale=factors[:, z, r : r + 1])
+                nc.vector.tensor_tensor(product[:, r, :], xf_rows[z][r][:].indirect(xf_list[:]), xb_scaled[:], ALU.mult)
+
+            codes, scales = [], []
+            for h in range(HALVES):
+                woven = keep.tile([P, P, PACK], BF16, name="woven%d_%d" % (z, h), align_bytes=64)
+                source = product[:, :, h * P : (h + 1) * P].rearrange("p r j -> p j r")
+                if h == 0:
+                    nc.scalar.activation(woven[:], source, ACT.Copy)
+                else:
+                    nc.vector.tensor_copy(woven[:], source)
+                u_codes = keep.tile([P, P], U32, name="u_codes%d_%d" % (z, h), align_bytes=64)
+                u_scales = keep.tile([P, P], U8, name="u_scales%d_%d" % (z, h), align_bytes=64)
+                codes.append((woven, u_codes, u_scales))
+
+            if z == 0:
+                nc.scalar.activation(
+                    bias_scaled[:].rearrange("p (n c) -> p n c", c=2),
+                    bias_bank[:].rearrange("p c n -> p n c"),
+                    ACT.Copy,
+                    scale=-1.0 / I,
+                )
+                for zz in range(PASSES):
+                    ks = keep.tile([P, I], U8, name="picked_scales%d" % zz, align_bytes=64)
+                    nc.vector.tensor_copy(ks[:], key_scales[:, zz, :].indirect(ky_list[:]))
+                    picked_scales.append(ks)
+            for h in reversed(range(HALVES)):
+                woven, u_codes, u_scales = codes[h]
+                nc.vector.quantize_mx(
+                    out=u_codes[:].bitcast(E5M2X4), scales=u_scales[:], in_=woven[:].rearrange("p j r -> p (j r)")
+                )
+            scales.append(0)
+            picked_scales.append(codes)
+
+        for z in range(PASSES):
+            picked_words = keep.tile([P, I], U32, name="picked_words%d" % z, align_bytes=64)
+            nc.vector.tensor_copy(picked_words[:], key_words[z][:].bitcast(U32).indirect(ky_list[:]))
+            for h in range(HALVES):
+                woven, u_codes, u_scales = picked_scales[PASSES + z][h]
+                nc.tensor.matmul_mx(
+                    acc[h][:],
+                    lhsT=u_codes[:].bitcast(E5M2X4),
+                    lhsT_scale=u_scales[:],
+                    rhs=picked_words[:].bitcast(E4M3X4),
+                    rhs_scale=picked_scales[z][:],
+                    start=(z == 0),
+                    stop=(z == PASSES - 1),
+                )
+
+        for h in range(HALVES):
+            scaled = keep.tile([P, I], F32, name="scaled%d" % h)
+            neg_mean = keep.tile([P, 1], F32, name="neg_mean%d" % h)
+            nc.vector.scalar_tensor_tensor(
+                scaled[:], acc[h][:], -1.0 / I, bias_scaled[:], ALU.mult, ALU.add, accum_out=neg_mean[:]
+            )
+            result = keep.tile([P, I], F32, name="result%d" % h)
+            nc.scalar.activation(result[:], scaled[:], ACT.Relu, bias=neg_mean[:], scale=-float(I))
+            queue = nc.sync if h == 0 else nc.scalar
+            queue.dma_start(out[h * P : (h + 1) * P, :], result[:])

@@ -36,100 +36,137 @@ def tile_list_scores_products_listed_abovemean_kernel(tc, xf, xb, fk, ky_words, 
         xb_list = keep.tile([P, J // 16], U16, name="xb_list")
         ky_list = keep.tile([P, I // 16], U16, name="ky_list")
         factors = keep.tile([P, PASSES, 2 * PACK], F32, name="factors")
-        xb_rows = [keep.tile([P, PACK, S], F32, name="xb_rows%d" % z) for z in range(PASSES)]
+        xb_rows = [[keep.tile([P, 2, S], F32, name="xb_rows%d_%d" % (z, c)) for c in range(2)] for z in range(PASSES)]
         xf_rows = [[keep.tile([P, T], F32, name="xf_rows%d_%d" % (z, r)) for r in range(PACK)] for z in range(PASSES)]
-        key_words = [keep.tile([P, V], I32, name="key_words%d" % z) for z in range(PASSES)]
+        key_words = [keep.tile([P, V], I32, name="key_words%d" % z, tag="words%d" % z, align_bytes=64) for z in range(PASSES)]
         key_scales = keep.tile([P, PASSES, V], U8, name="key_scales")
         bias_pairs = keep.tile([P, 2], F32, name="bias_pairs")
         identity = keep.tile([P, P], F32, name="identity")
 
         xf_view = xf.rearrange("(z p r) t -> z r p t", z=PASSES, r=PACK)
-        xb_view = xb.rearrange("(z p r) s -> z p r s", z=PASSES, r=PACK)
-
-        nc.sync.dma_start(xb_rows[0][:], xb_view[0])
-        nc.sync.dma_start(xb_list[:], offs2)
-        nc.sync.dma_start(factors[:, :, 0:PACK], fk.rearrange("(z p r) o -> p z (r o)", z=PASSES, r=PACK))
-        nc.sync.dma_start(xf_rows[0][0][:], xf_view[0, 0])
-        nc.sync.dma_start(xf_list[:], offs)
-        for r in range(1, PACK):
-            nc.sync.dma_start(xf_rows[0][r][:], xf_view[0, r])
-        nc.sync.dma_start(xb_rows[1][:], xb_view[1])
-        nc.sync.dma_start(ky_list[:], offs3)
-        for r in range(PACK):
-            nc.sync.dma_start(xf_rows[1][r][:], xf_view[1, r])
-        for z in range(PASSES):
-            nc.sync.dma_start(key_words[z][:], ky_words[z].rearrange("p n r -> p (n r)").bitcast(I32))
+        xb_view = xb.rearrange("(z p c e) s -> z c p e s", z=PASSES, c=2, e=2)
 
         nc.vector.memset(key_scales[:].rearrange("p z v -> p (z v)").bitcast(I32), 0)
-        for q in range(QUADRANTS):
-            nc.gpsimd.dma_start(
+        make_identity(nc, identity[:])
+
+        def load_xf(z, r):
+            nc.sync.dma_start(xf_rows[z][r][:], xf_view[z, r])
+
+        def load_xb(z, c):
+            nc.sync.dma_start(xb_rows[z][c][:], xb_view[z, c])
+
+        def load_words(z):
+            nc.sync.dma_start(key_words[z][:], ky_words[z].rearrange("p n r -> p (n r)").bitcast(I32))
+
+        def load_scales(q):
+            nc.sync.dma_start(
                 key_scales[32 * q : 32 * q + SCALE_ROWS].bitcast(I32),
                 ky_scales[:, SCALE_ROWS * q : SCALE_ROWS * (q + 1), :].rearrange("z r v -> r z v").bitcast(I32),
             )
-        nc.gpsimd.dma_start(bias_pairs[:], bi.rearrange("o (p c) -> p (o c)", c=2))
-        make_identity(nc, identity[:])
 
+        def load_bias():
+            nc.sync.dma_start(bias_pairs[:], bi.rearrange("o (p c) -> p (o c)", c=2))
+
+        def load_factors():
+            nc.sync.dma_start(factors[:, :, 0:PACK], fk.rearrange("(z p r) o -> p z (r o)", z=PASSES, r=PACK))
+
+        load_xb(0, 0)
+        nc.sync.dma_start(xb_list[:], offs2)
+        load_factors()
+        load_xf(0, 0)
+        nc.sync.dma_start(xf_list[:], offs)
+        load_xb(0, 1)
+        load_xf(0, 1)
+        nc.sync.dma_start(ky_list[:], offs3)
+        for q in range(QUADRANTS):
+            load_scales(q)
+        load_xf(0, 2)
+        load_xb(1, 0)
+        load_xf(0, 3)
+        load_xb(1, 1)
+        load_bias()
+        for r in range(PACK):
+            load_xf(1, r)
+        load_words(0)
+        load_words(1)
+
+        product = [keep.tile([P, PACK, J], F32, name="product%d" % z) for z in range(PASSES)]
+        woven = [[keep.tile([P, P, PACK], BF16, name="woven%d_%d" % (z, h), align_bytes=64) for h in range(HALVES)] for z in range(PASSES)]
+        u_codes = {}
+        u_scales = [[keep.tile([P, P], U8, name="u_scales%d_%d" % (z, h), align_bytes=64) for h in range(HALVES)] for z in range(PASSES)]
+        picked_scales = [keep.tile([P, I], U8, name="picked_scales%d" % z, align_bytes=64) for z in range(PASSES)]
+        picked_words = [keep.tile([P, I], U32, name="picked_words%d" % z, align_bytes=64) for z in range(PASSES)]
+        acc = [psum.tile([P, I], F32, name="acc%d" % h) for h in range(HALVES)]
         bias_bank = psum.tile([P, 2, P], F32, name="bias_bank")
-        for c in range(2):
-            nc.tensor.transpose(bias_bank[:, c, :], bias_pairs[:, c : c + 1].to_broadcast([P, P]), identity[:])
         bias_scaled = keep.tile([P, I], F32, name="bias_scaled")
 
-        acc = [psum.tile([P, I], F32, name="acc%d" % h) for h in range(HALVES)]
-        picked_scales = []
-        for z in range(PASSES):
-            product = keep.tile([P, PACK, J], F32, name="product%d" % z)
-            for r in range(PACK):
-                xb_picked = keep.tile([P, J], F32, name="xb_picked%d_%d" % (z, r))
-                nc.scalar.activation(xb_picked[:], xb_rows[z][:, r, :].indirect(xb_list[:]), ACT.Copy)
-                xb_scaled = keep.tile([P, J], F32, name="xb_scaled%d_%d" % (z, r))
-                nc.scalar.activation(xb_scaled[:], xb_picked[:], ACT.Copy, scale=factors[:, z, r : r + 1])
-                nc.vector.tensor_tensor(product[:, r, :], xf_rows[z][r][:].indirect(xf_list[:]), xb_scaled[:], ALU.mult)
+        def spread_bias():
+            for c in range(2):
+                nc.tensor.transpose(bias_bank[:, c, :], bias_pairs[:, c : c + 1].to_broadcast([P, P]), identity[:])
+            nc.scalar.activation(
+                bias_scaled[:].rearrange("p (n c) -> p n c", c=2),
+                bias_bank[:].rearrange("p c n -> p n c"),
+                ACT.Copy,
+                scale=-1.0 / I,
+            )
 
-            codes, scales = [], []
+        def multiply_rows(z, r):
+            xb_picked = keep.tile([P, J], F32, name="xb_picked%d_%d" % (z, r))
+            nc.scalar.activation(xb_picked[:], xb_rows[z][r // 2][:, r % 2, :].indirect(xb_list[:]), ACT.Copy)
+            xb_scaled = keep.tile([P, J], F32, name="xb_scaled%d_%d" % (z, r))
+            nc.scalar.activation(xb_scaled[:], xb_picked[:], ACT.Copy, scale=factors[:, z, r : r + 1])
+            nc.vector.tensor_tensor(product[z][:, r, :], xf_rows[z][r][:].indirect(xf_list[:]), xb_scaled[:], ALU.mult)
+
+        def weave(z):
+            halves = [product[z][:, :, h * P : (h + 1) * P].rearrange("p r j -> p j r") for h in range(HALVES)]
+            nc.scalar.activation(woven[z][1][:], halves[1], ACT.Copy)
+            nc.vector.tensor_copy(woven[z][0][:], halves[0])
+
+        def quantise(z, h, tag):
+            u_codes[z, h] = keep.tile([P, P], U32, name="u_codes%d_%d" % (z, h), tag=tag, align_bytes=64)
+            nc.vector.quantize_mx(
+                out=u_codes[z, h][:].bitcast(E5M2X4),
+                scales=u_scales[z][h][:],
+                in_=woven[z][h][:].rearrange("p j r -> p (j r)"),
+            )
+
+        def pick_scales(z):
+            nc.vector.tensor_copy(picked_scales[z][:], key_scales[:, z, :].indirect(ky_list[:]))
+
+        def pick_words(z):
+            nc.vector.tensor_copy(picked_words[z][:], key_words[z][:].bitcast(U32).indirect(ky_list[:]))
+
+        def contract(z):
             for h in range(HALVES):
-                woven = keep.tile([P, P, PACK], BF16, name="woven%d_%d" % (z, h), align_bytes=64)
-                source = product[:, :, h * P : (h + 1) * P].rearrange("p r j -> p j r")
-                if h == 0:
-                    nc.scalar.activation(woven[:], source, ACT.Copy)
-                else:
-                    nc.vector.tensor_copy(woven[:], source)
-                u_codes = keep.tile([P, P], U32, name="u_codes%d_%d" % (z, h), align_bytes=64)
-                u_scales = keep.tile([P, P], U8, name="u_scales%d_%d" % (z, h), align_bytes=64)
-                codes.append((woven, u_codes, u_scales))
-
-            if z == 0:
-                nc.scalar.activation(
-                    bias_scaled[:].rearrange("p (n c) -> p n c", c=2),
-                    bias_bank[:].rearrange("p c n -> p n c"),
-                    ACT.Copy,
-                    scale=-1.0 / I,
-                )
-                for zz in range(PASSES):
-                    ks = keep.tile([P, I], U8, name="picked_scales%d" % zz, align_bytes=64)
-                    nc.vector.tensor_copy(ks[:], key_scales[:, zz, :].indirect(ky_list[:]))
-                    picked_scales.append(ks)
-            for h in reversed(range(HALVES)):
-                woven, u_codes, u_scales = codes[h]
-                nc.vector.quantize_mx(
-                    out=u_codes[:].bitcast(E5M2X4), scales=u_scales[:], in_=woven[:].rearrange("p j r -> p (j r)")
-                )
-            scales.append(0)
-            picked_scales.append(codes)
-
-        for z in range(PASSES):
-            picked_words = keep.tile([P, I], U32, name="picked_words%d" % z, align_bytes=64)
-            nc.vector.tensor_copy(picked_words[:], key_words[z][:].bitcast(U32).indirect(ky_list[:]))
-            for h in range(HALVES):
-                woven, u_codes, u_scales = picked_scales[PASSES + z][h]
                 nc.tensor.matmul_mx(
                     acc[h][:],
-                    lhsT=u_codes[:].bitcast(E5M2X4),
-                    lhsT_scale=u_scales[:],
-                    rhs=picked_words[:].bitcast(E4M3X4),
+                    lhsT=u_codes[z, h][:].bitcast(E5M2X4),
+                    lhsT_scale=u_scales[z][h][:],
+                    rhs=picked_words[z][:].bitcast(E4M3X4),
                     rhs_scale=picked_scales[z][:],
                     start=(z == 0),
                     stop=(z == PASSES - 1),
                 )
+
+        multiply_rows(0, 0)
+        multiply_rows(0, 1)
+        pick_scales(0)
+        pick_scales(1)
+        multiply_rows(0, 2)
+        multiply_rows(0, 3)
+        weave(0)
+        quantise(0, 0, "codes0")
+        quantise(0, 1, "codes1")
+        for r in range(PACK):
+            multiply_rows(1, r)
+        spread_bias()
+        weave(1)
+        pick_words(0)
+        contract(0)
+        quantise(1, 0, "words0")
+        pick_words(1)
+        quantise(1, 1, "words1")
+        contract(1)
 
         for h in range(HALVES):
             scaled = keep.tile([P, I], F32, name="scaled%d" % h)

@@ -36,33 +36,31 @@ def tile_list_scores_products_listed_abovemean_kernel(tc, xf, xb, fk, ky_words, 
         xb_list = keep.tile([P, J // 16], U16, name="xb_list")
         ky_list = keep.tile([P, I // 16], U16, name="ky_list")
         factors = keep.tile([P, PASSES, 2 * PACK], F32, name="factors")
-        xb_rows = [[keep.tile([P, 2, S], F32, name="xb_rows%d_%d" % (z, c)) for c in range(2)] for z in range(PASSES)]
-        xf_rows = [[keep.tile([P, T], F32, name="xf_rows%d_%d" % (z, r)) for r in range(PACK)] for z in range(PASSES)]
+        xb_rows = [keep.tile([P, PACK, S], F32, name="xb_rows%d" % z) for z in range(PASSES)]
+        xf_rows = {}
         key_words = [keep.tile([P, V], I32, name="key_words%d" % z, tag="words%d" % z, align_bytes=64) for z in range(PASSES)]
         key_scales = keep.tile([P, PASSES, V], U8, name="key_scales")
         bias_pairs = keep.tile([P, 2], F32, name="bias_pairs")
         identity = keep.tile([P, P], F32, name="identity")
 
-        xf_view = xf.rearrange("(z p r) t -> z r p t", z=PASSES, r=PACK)
-        xb_view = xb.rearrange("(z p c e) s -> z c p e s", z=PASSES, c=2, e=2)
+        xf_view = xf.rearrange("(z p r) t -> z p (r t)", z=PASSES, r=PACK)
+        xb_view = xb.rearrange("(z p r) s -> z p r s", z=PASSES, r=PACK)
 
         nc.vector.memset(key_scales[:].rearrange("p z v -> p (z v)").bitcast(I32), 0)
         make_identity(nc, identity[:])
 
-        def load_xf(z, r):
-            nc.sync.dma_start(xf_rows[z][r][:], xf_view[z, r])
+        def load_xf(z, r, count):
+            xf_rows[z, r] = keep.tile([P, count * T], F32, name="xf_rows%d_%d" % (z, r))
+            nc.sync.dma_start(xf_rows[z, r][:], xf_view[z][:, r * T : (r + count) * T])
 
-        def load_xb(z, c):
-            nc.sync.dma_start(xb_rows[z][c][:], xb_view[z, c])
+        def load_xb(z):
+            nc.sync.dma_start(xb_rows[z][:], xb_view[z])
 
         def load_words(z):
             nc.sync.dma_start(key_words[z][:], ky_words[z].rearrange("p n r -> p (n r)").bitcast(I32))
 
-        def load_scales(q):
-            nc.sync.dma_start(
-                key_scales[32 * q : 32 * q + SCALE_ROWS].bitcast(I32),
-                ky_scales[:, SCALE_ROWS * q : SCALE_ROWS * (q + 1), :].rearrange("z r v -> r z v").bitcast(I32),
-            )
+        def load_scales():
+            nc.sync.dma_start(key_scales[0:P:8].bitcast(I32), ky_scales.rearrange("z q v -> q z v").bitcast(I32))
 
         def load_bias():
             nc.sync.dma_start(bias_pairs[:], bi.rearrange("o (p c) -> p (o c)", c=2))
@@ -70,23 +68,19 @@ def tile_list_scores_products_listed_abovemean_kernel(tc, xf, xb, fk, ky_words, 
         def load_factors():
             nc.sync.dma_start(factors[:, :, 0:PACK], fk.rearrange("(z p r) o -> p z (r o)", z=PASSES, r=PACK))
 
-        load_xb(0, 0)
+        load_xb(0)
+        nc.sync.dma_start(ky_list[:], offs3)
+        load_scales()
         nc.sync.dma_start(xb_list[:], offs2)
         load_factors()
-        load_xf(0, 0)
+        load_xf(0, 0, 2)
         nc.sync.dma_start(xf_list[:], offs)
-        load_xb(0, 1)
-        load_xf(0, 1)
-        nc.sync.dma_start(ky_list[:], offs3)
-        for q in range(QUADRANTS):
-            load_scales(q)
-        load_xf(0, 2)
-        load_xb(1, 0)
-        load_xf(0, 3)
-        load_xb(1, 1)
+        load_xb(1)
+        load_xf(0, 2, 2)
         load_bias()
-        for r in range(PACK):
-            load_xf(1, r)
+        load_xf(1, 0, 2)
+        load_xf(1, 2, 1)
+        load_xf(1, 3, 1)
         load_words(0)
         load_words(1)
 
@@ -94,7 +88,9 @@ def tile_list_scores_products_listed_abovemean_kernel(tc, xf, xb, fk, ky_words, 
         woven = [[keep.tile([P, P, PACK], BF16, name="woven%d_%d" % (z, h), align_bytes=64) for h in range(HALVES)] for z in range(PASSES)]
         u_codes = {}
         u_scales = [[keep.tile([P, P], U8, name="u_scales%d_%d" % (z, h), align_bytes=64) for h in range(HALVES)] for z in range(PASSES)]
-        picked_scales = [keep.tile([P, I], U8, name="picked_scales%d" % z, align_bytes=64) for z in range(PASSES)]
+        picked_scales = keep.tile([P, PASSES, I], U8, name="picked_scales")
+        key_planes = keep.tile([P, PASSES, I], U8, name="key_planes", align_bytes=64)
+        nc.vector.memset(key_planes[:].rearrange("p z i -> p (z i)").bitcast(I32), 0)
         picked_words = [keep.tile([P, I], U32, name="picked_words%d" % z, align_bytes=64) for z in range(PASSES)]
         acc = [psum.tile([P, I], F32, name="acc%d" % h) for h in range(HALVES)]
         bias_bank = psum.tile([P, 2, P], F32, name="bias_bank")
@@ -112,10 +108,23 @@ def tile_list_scores_products_listed_abovemean_kernel(tc, xf, xb, fk, ky_words, 
 
         def multiply_rows(z, r):
             xb_picked = keep.tile([P, J], F32, name="xb_picked%d_%d" % (z, r))
-            nc.scalar.activation(xb_picked[:], xb_rows[z][r // 2][:, r % 2, :].indirect(xb_list[:]), ACT.Copy)
+            nc.scalar.activation(xb_picked[:], xb_rows[z][:, r, :].indirect(xb_list[:]), ACT.Copy)
             xb_scaled = keep.tile([P, J], F32, name="xb_scaled%d_%d" % (z, r))
             nc.scalar.activation(xb_scaled[:], xb_picked[:], ACT.Copy, scale=factors[:, z, r : r + 1])
-            nc.vector.tensor_tensor(product[z][:, r, :], xf_rows[z][r][:].indirect(xf_list[:]), xb_scaled[:], ALU.mult)
+            nc.vector.tensor_tensor(product[z][:, r, :], xf_rows[z, r][:].indirect(xf_list[:]), xb_scaled[:], ALU.mult)
+
+        def multiply_second_rows(z, r, on_vector):
+            xb_picked = keep.tile([P, J], F32, name="xb_picked%d_%d" % (z, r))
+            nc.scalar.activation(xb_picked[:], xb_rows[z][:, r, :].indirect(xb_list[:]), ACT.Copy)
+            xf_picked = keep.tile([P, J], F32, name="xf_picked%d_%d" % (z, r))
+            window = xf_rows[z, r - 1][:, T : 2 * T].indirect(xf_list[:])
+            if on_vector:
+                nc.vector.tensor_copy(xf_picked[:], window)
+            else:
+                nc.scalar.activation(xf_picked[:], window, ACT.Copy)
+            nc.vector.scalar_tensor_tensor(
+                product[z][:, r, :], xf_picked[:], factors[:, z, r : r + 1], xb_picked[:], ALU.mult, ALU.mult
+            )
 
         def weave(z):
             halves = [product[z][:, :, h * P : (h + 1) * P].rearrange("p r j -> p j r") for h in range(HALVES)]
@@ -131,7 +140,14 @@ def tile_list_scores_products_listed_abovemean_kernel(tc, xf, xb, fk, ky_words, 
             )
 
         def pick_scales(z):
-            nc.vector.tensor_copy(picked_scales[z][:], key_scales[:, z, :].indirect(ky_list[:]))
+            nc.vector.tensor_copy(picked_scales[:, z, :], key_scales[:, z, :].indirect(ky_list[:]))
+
+        def place_scales():
+            for r in range(SCALE_ROWS):
+                nc.gpsimd.dma_start(
+                    key_planes[r:P:32].rearrange("p z i -> p (z i)").bitcast(I32),
+                    picked_scales[8 * r : P : 32].rearrange("p z i -> p (z i)").bitcast(I32),
+                )
 
         def pick_words(z):
             nc.vector.tensor_copy(picked_words[z][:], key_words[z][:].bitcast(U32).indirect(ky_list[:]))
@@ -143,22 +159,25 @@ def tile_list_scores_products_listed_abovemean_kernel(tc, xf, xb, fk, ky_words, 
                     lhsT=u_codes[z, h][:].bitcast(E5M2X4),
                     lhsT_scale=u_scales[z][h][:],
                     rhs=picked_words[z][:].bitcast(E4M3X4),
-                    rhs_scale=picked_scales[z][:],
+                    rhs_scale=key_planes[:, z, :],
                     start=(z == 0),
                     stop=(z == PASSES - 1),
                 )
 
-        multiply_rows(0, 0)
-        multiply_rows(0, 1)
         pick_scales(0)
         pick_scales(1)
+        place_scales()
+        multiply_rows(0, 0)
+        multiply_second_rows(0, 1, True)
         multiply_rows(0, 2)
-        multiply_rows(0, 3)
+        multiply_second_rows(0, 3, True)
         weave(0)
         quantise(0, 0, "codes0")
         quantise(0, 1, "codes1")
-        for r in range(PACK):
-            multiply_rows(1, r)
+        multiply_rows(1, 0)
+        multiply_second_rows(1, 1, False)
+        multiply_rows(1, 2)
+        multiply_rows(1, 3)
         spread_bias()
         weave(1)
         pick_words(0)

from contextlib import ExitStack

import concourse.mybir as mybir
from concourse.masks import make_identity

K, T, S, V, J, I = 1024, 1024, 512, 1024, 256, 256
FLOPS = 2 * K * J * I

F32 = mybir.dt.float32
BF16 = mybir.dt.bfloat16
I32 = mybir.dt.int32
U32 = mybir.dt.uint32
U16 = mybir.dt.uint16
U8 = mybir.dt.uint8
E4M3X4 = mybir.dt.float8_e4m3fn_x4
E5M2X4 = mybir.dt.float8_e5m2_x4
ALU = mybir.AluOpType
ACT = mybir.ActivationFunctionType

P = 128
PACK = 4
K_PASS = P * PACK
PASSES = K // K_PASS
HALVES = J // P
QUADRANTS = 4
SCALE_ROWS = 4


def tile_list_scores_products_listed_abovemean_kernel(tc, xf, xb, fk, ky_words, ky_scales, bi, offs, offs2, offs3, out):
    nc = tc.nc
    with ExitStack() as ctx:
        keep = ctx.enter_context(tc.tile_pool(name="keep", bufs=1))
        psum = ctx.enter_context(tc.psum_pool(name="psum", bufs=1))

        xf_list = keep.tile([P, J // 16], U16, name="xf_list")
        xb_list = keep.tile([P, J // 16], U16, name="xb_list")
        ky_list = keep.tile([P, I // 16], U16, name="ky_list")
        factors = keep.tile([P, PASSES, 2 * PACK], F32, name="factors")
        xb_rows = [keep.tile([P, PACK, S], F32, name="xb_rows%d" % z) for z in range(PASSES)]
        xf_rows = {}
        key_words = [keep.tile([P, V], I32, name="key_words%d" % z, tag="words%d" % z, align_bytes=64) for z in range(PASSES)]
        key_scales = keep.tile([P, PASSES, V], U8, name="key_scales")
        bias_pairs = keep.tile([P, 2], F32, name="bias_pairs")
        identity = keep.tile([P, P], F32, name="identity")

        xf_view = xf.rearrange("(z p r) t -> z p (r t)", z=PASSES, r=PACK)
        xb_view = xb.rearrange("(z p r) s -> z p r s", z=PASSES, r=PACK)

        nc.vector.memset(key_scales[:].rearrange("p z v -> p (z v)").bitcast(I32), 0)
        make_identity(nc, identity[:])

        def load_xf(z, r, count):
            xf_rows[z, r] = keep.tile([P, count * T], F32, name="xf_rows%d_%d" % (z, r))
            nc.sync.dma_start(xf_rows[z, r][:], xf_view[z][:, r * T : (r + count) * T])

        def load_xb(z):
            nc.sync.dma_start(xb_rows[z][:], xb_view[z])

        def load_words(z):
            nc.sync.dma_start(key_words[z][:], ky_words[z].rearrange("p n r -> p (n r)").bitcast(I32))

        def load_scales():
            nc.sync.dma_start(key_scales[0:P:8].bitcast(I32), ky_scales.rearrange("z q v -> q z v").bitcast(I32))

        def load_bias():
            nc.sync.dma_start(bias_pairs[:], bi.rearrange("o (p c) -> p (o c)", c=2))

        def load_factors():
            nc.sync.dma_start(factors[:, :, 0:PACK], fk.rearrange("(z p r) o -> p z (r o)", z=PASSES, r=PACK))

        load_xb(0)
        nc.sync.dma_start(ky_list[:], offs3)
        load_scales()
        nc.sync.dma_start(xb_list[:], offs2)
        load_factors()
        load_xf(0, 0, 2)
        nc.sync.dma_start(xf_list[:], offs)
        load_xb(1)
        load_xf(0, 2, 2)
        load_bias()
        load_xf(1, 0, 2)
        load_xf(1, 2, 1)
        load_xf(1, 3, 1)
        load_words(0)
        load_words(1)

        product = [keep.tile([P, PACK, J], F32, name="product%d" % z) for z in range(PASSES)]
        woven = [[keep.tile([P, P, PACK], BF16, name="woven%d_%d" % (z, h), align_bytes=64) for h in range(HALVES)] for z in range(PASSES)]
        u_codes = {}
        u_scales = [[keep.tile([P, P], U8, name="u_scales%d_%d" % (z, h), align_bytes=64) for h in range(HALVES)] for z in range(PASSES)]
        picked_scales = keep.tile([P, PASSES, I], U8, name="picked_scales")
        key_planes = keep.tile([P, PASSES, I], U8, name="key_planes", align_bytes=64)
        nc.vector.memset(key_planes[:].rearrange("p z i -> p (z i)").bitcast(I32), 0)
        picked_words = [keep.tile([P, I], U32, name="picked_words%d" % z, align_bytes=64) for z in range(PASSES)]
        acc = [psum.tile([P, I], F32, name="acc%d" % h) for h in range(HALVES)]
        bias_bank = psum.tile([P, 2, P], F32, name="bias_bank")
        bias_scaled = keep.tile([P, I], F32, name="bias_scaled")

        def spread_bias():
            for c in range(2):
                nc.tensor.transpose(bias_bank[:, c, :], bias_pairs[:, c : c + 1].to_broadcast([P, P]), identity[:])
            nc.scalar.activation(
                bias_scaled[:].rearrange("p (n c) -> p n c", c=2),
                bias_bank[:].rearrange("p c n -> p n c"),
                ACT.Copy,
                scale=-1.0 / I,
            )

        def multiply_rows(z, r):
            xb_picked = keep.tile([P, J], F32, name="xb_picked%d_%d" % (z, r))
            nc.scalar.activation(xb_picked[:], xb_rows[z][:, r, :].indirect(xb_list[:]), ACT.Copy)
            xb_scaled = keep.tile([P, J], F32, name="xb_scaled%d_%d" % (z, r))
            nc.scalar.activation(xb_scaled[:], xb_picked[:], ACT.Copy, scale=factors[:, z, r : r + 1])
            nc.vector.tensor_tensor(product[z][:, r, :], xf_rows[z, r][:].indirect(xf_list[:]), xb_scaled[:], ALU.mult)

        def multiply_second_rows(z, r, on_vector):
            xb_picked = keep.tile([P, J], F32, name="xb_picked%d_%d" % (z, r))
            nc.scalar.activation(xb_picked[:], xb_rows[z][:, r, :].indirect(xb_list[:]), ACT.Copy)
            xf_picked = keep.tile([P, J], F32, name="xf_picked%d_%d" % (z, r))
            window = xf_rows[z, r - 1][:, T : 2 * T].indirect(xf_list[:])
            if on_vector:
                nc.vector.tensor_copy(xf_picked[:], window)
            else:
                nc.scalar.activation(xf_picked[:], window, ACT.Copy)
            nc.vector.scalar_tensor_tensor(
                product[z][:, r, :], xf_picked[:], factors[:, z, r : r + 1], xb_picked[:], ALU.mult, ALU.mult
            )

        def weave(z):
            halves = [product[z][:, :, h * P : (h + 1) * P].rearrange("p r j -> p j r") for h in range(HALVES)]
            nc.scalar.activation(woven[z][1][:], halves[1], ACT.Copy)
            nc.vector.tensor_copy(woven[z][0][:], halves[0])

        def quantise(z, h, tag):
            u_codes[z, h] = keep.tile([P, P], U32, name="u_codes%d_%d" % (z, h), tag=tag, align_bytes=64)
            nc.vector.quantize_mx(
                out=u_codes[z, h][:].bitcast(E5M2X4),
                scales=u_scales[z][h][:],
                in_=woven[z][h][:].rearrange("p j r -> p (j r)"),
            )

        def pick_scales(z):
            nc.vector.tensor_copy(picked_scales[:, z, :], key_scales[:, z, :].indirect(ky_list[:]))

        def place_scales():
            for r in range(SCALE_ROWS):
                nc.gpsimd.dma_start(
                    key_planes[r:P:32].rearrange("p z i -> p (z i)").bitcast(I32),
                    picked_scales[8 * r : P : 32].rearrange("p z i -> p (z i)").bitcast(I32),
                )

        def pick_words(z):
            nc.vector.tensor_copy(picked_words[z][:], key_words[z][:].bitcast(U32).indirect(ky_list[:]))

        def contract(z):
            for h in range(HALVES):
                nc.tensor.matmul_mx(
                    acc[h][:],
                    lhsT=u_codes[z, h][:].bitcast(E5M2X4),
                    lhsT_scale=u_scales[z][h][:],
                    rhs=picked_words[z][:].bitcast(E4M3X4),
                    rhs_scale=key_planes[:, z, :],
                    start=(z == 0),
                    stop=(z == PASSES - 1),
                )

        pick_scales(0)
        pick_scales(1)
        place_scales()
        multiply_rows(0, 0)
        multiply_second_rows(0, 1, True)
        multiply_rows(0, 2)
        multiply_second_rows(0, 3, True)
        weave(0)
        quantise(0, 0, "codes0")
        quantise(0, 1, "codes1")
        multiply_rows(1, 0)
        multiply_second_rows(1, 1, False)
        multiply_rows(1, 2)
        multiply_rows(1, 3)
        spread_bias()
        weave(1)
        pick_words(0)
        contract(0)
        quantise(1, 0, "words0")
        pick_words(1)
        quantise(1, 1, "words1")
        contract(1)

        for h in range(HALVES):
            scaled = keep.tile([P, I], F32, name="scaled%d" % h)
            neg_mean = keep.tile([P, 1], F32, name="neg_mean%d" % h)
            nc.vector.scalar_tensor_tensor(
                scaled[:], acc[h][:], -1.0 / I, bias_scaled[:], ALU.mult, ALU.add, accum_out=neg_mean[:]
            )
            result = keep.tile([P, I], F32, name="result%d" % h)
            nc.scalar.activation(result[:], scaled[:], ACT.Relu, bias=neg_mean[:], scale=-float(I))
            queue = nc.sync if h == 0 else nc.scalar
            queue.dma_start(out[h * P : (h + 1) * P, :], result[:])
